import numpy as np
import ml_dtypes


def mxq(x, axis, fmt="e4m3"):
    dtype, down = {"e4m3": (ml_dtypes.float8_e4m3fn, 7), "e5m2": (ml_dtypes.float8_e5m2, 14)}[fmt]
    v = np.moveaxis(np.asarray(x, np.float32).astype(ml_dtypes.bfloat16).astype(np.float64), axis, -1)
    blocks = v.reshape(v.shape[:-1] + (-1, 32))
    amax = np.abs(blocks).max(-1, keepdims=True)
    byte = np.maximum(np.where(amax > 0, np.frexp(amax)[1] - 1 + 127, 0) - down, 1)
    scale = np.exp2(byte - 127.0)
    codes = (blocks / scale).astype(np.float32).astype(dtype).astype(np.float64)
    return np.moveaxis((codes * scale).reshape(v.shape), -1, axis)


WIDE = False


def mx_kscale(k):
    if not WIDE:
        return np.ones(k)
    levels = np.array([30, -30])
    if k % 512:
        return np.exp2(np.random.permutation(np.resize(levels, k // 32))).repeat(32)
    a = np.empty((k // 512, 16))
    for p in range(k // 512):
        a[p, :8] = np.random.permutation(np.resize(levels, 8))
        for g in range(8):
            far = levels[np.abs(levels - a[p, g]) >= 10]
            a[p, g + 8] = far[np.random.randint(len(far))]
    return np.exp2(a.ravel()).repeat(32)


def f64(x):
    return np.asarray(x).astype(np.float64)


def striped(idx):
    return np.tile(np.asarray(idx).reshape(-1, 16).T, (8, 1)).astype(np.uint16)


def unstriped(offs):
    return offs[:16].T.reshape(-1).astype(np.int64)


E2M1 = np.array([0.0, 0.5, 1.0, 1.5, 2.0, 3.0, 4.0, 6.0, -0.0, -0.5, -1.0, -1.5, -2.0, -3.0, -4.0, -6.0])


def pack_weight(w, fmt):
    k, n = w.shape
    w = f64(np.asarray(w, np.float32).astype(ml_dtypes.bfloat16)).reshape(k // 32, 32, n)
    amax = np.abs(w).max(1)
    if fmt == "e4m3":
        byte = np.frexp(amax)[1] - 1 + 127 - 7
    else:
        mant, ex = np.frexp(amax / 6.0)
        byte = np.where(mant > 0.5, ex, ex - 1) + 127
    byte = np.clip(np.where(amax > 0, byte, 1), 1, 254)
    scaled = (w * np.exp2(127.0 - byte)[:, None, :]).reshape(k, n).astype(np.float32)
    by_word = np.ascontiguousarray(scaled.reshape(k // 512, 128, 4, n).transpose(0, 1, 3, 2))
    if fmt == "e4m3":
        words = by_word.astype(ml_dtypes.float8_e4m3fn).view(np.uint8)
    else:
        c = by_word.astype(ml_dtypes.float4_e2m1fn).view(np.uint8) & 0xF
        words = (c[..., 0::2] | (c[..., 1::2] << 4)).reshape(k // 512, 128, 2 * n)
    return np.ascontiguousarray(words), np.ascontiguousarray(byte.astype(np.uint8).reshape(k // 512, 16, n))


def unpack_weight(words, scales, fmt):
    g, _, n = scales.shape
    words = np.ascontiguousarray(words).reshape(g, 128, n, -1)
    if fmt == "e4m3":
        vals = words.view(ml_dtypes.float8_e4m3fn).astype(np.float64)
    else:
        nib = np.empty((g, 128, n, 4), np.uint8)
        nib[..., 0::2] = words & 0xF
        nib[..., 1::2] = words >> 4
        vals = E2M1[nib]
    vals = vals * np.repeat(np.exp2(scales.astype(np.float64) - 127.0), 8, axis=1)[..., None]
    return vals.transpose(0, 1, 3, 2).reshape(g * 512, n)


def bf(x):
    return np.asarray(x, np.float32).astype(ml_dtypes.bfloat16)


def planes(Y):
    r, m = Y.shape
    b = f64(bf(Y)).reshape(r // 32, 32, m)
    amax = np.abs(b).max(1)
    byte = np.clip(np.where(amax > 0, np.frexp(amax)[1] - 1 + 127 - 7, 1), 1, 254)
    codes = (b * np.exp2(127.0 - byte)[:, None, :]).reshape(r, m).astype(np.float32).astype(ml_dtypes.float8_e4m3fn).view(np.uint8)
    words = codes.reshape(r // 512, 128, 4, m).transpose(0, 1, 3, 2)
    return np.ascontiguousarray(words), np.ascontiguousarray(byte.astype(np.uint8).reshape(r // 512, 16, m))


K, R, N, T, J, V = 512, 512, 512, 1024, 512, 1024


def setup_inputs():
    n = np.random.standard_normal
    idx = np.random.permutation(T)[:J]
    idx2 = np.random.permutation(V)[:J]
    fn = mx_kscale(N)
    fr = mx_kscale(R)
    wdp = pack_weight(n((N, R)) * 1 / np.sqrt(N) * fn[:, None] * fr, "e4m3")
    wup = pack_weight(n((R, K)) * 1 / np.sqrt(R) / fr[:, None], "e2m1")
    return {
        "g": (n((N, T)) * np.exp(0.5 * n((1, T))) / fn[:, None]).astype(np.float32),
        "wd_words": wdp[0],
        "wd_scales": wdp[1],
        "tb": (n((R, V)) * 0.5 * fr[:, None]).astype(np.float32),
        "wu_words": wup[0],
        "wu_scales": wup[1],
        "offs": striped(idx),
        "offs2": striped(idx2),
    }


def reference(g, wd_words, wd_scales, tb, wu_words, wu_scales, offs, offs2):
    idx = unstriped(offs)
    idx2 = unstriped(offs2)
    wdu = unpack_weight(wd_words, wd_scales, "e4m3")
    wuu = unpack_weight(wu_words, wu_scales, "e2m1")
    gidxq = mxq(f64(g)[:, idx], 0, "e5m2")
    dh = wdu.T @ gidxq
    dz = dh - f64(tb)[:, idx2]
    dzq = mxq(dz, 0, "e5m2")
    y = wuu.T @ dzq
    words, scales = planes(y)
    return y, words, scales

@@ -1,0 +1,184 @@
+from contextlib import ExitStack
+
+import concourse.mybir as mybir
+
+F32 = mybir.dt.float32
+BF16 = mybir.dt.bfloat16
+I32 = mybir.dt.int32
+U32 = mybir.dt.uint32
+U16 = mybir.dt.uint16
+U8 = mybir.dt.uint8
+E4M3 = mybir.dt.float8_e4m3fn_x4
+E5M2 = mybir.dt.float8_e5m2_x4
+E2M1 = mybir.dt.float4_e2m1fn_x4
+COPY = mybir.ActivationFunctionType.Copy
+MULT = mybir.AluOpType.mult
+SUB = mybir.AluOpType.subtract
+
+P = 128
+PACK = 4
+T = 1024
+J = 512
+C = 512
+HALF_T = T // 2
+HALF_J = J // 2
+LAST_CAST_VECTOR = 352
+PAIR_VECTOR = 352
+
+FLOPS = 2 * 2 * 512 * 512 * 512
+
+
+def load_scale_rows(nc, queue, tile, rows):
+    nc.vector.memset(tile[:].bitcast(U32), 0)
+    for q in range(4):
+        queue.dma_start(out=tile[32 * q : 32 * q + 4, :].bitcast(I32), in_=rows[0, 4 * q : 4 * q + 4, :].bitcast(I32))
+
+
+def deal(nc, dealt, raw, b):
+    nc.vector.tensor_copy(
+        out=dealt.rearrange("p (t m b) -> p m t b", t=PACK, b=b),
+        in_=raw.rearrange("p (m t b) -> p m t b", t=PACK, b=b),
+    )
+
+
+def tile_list_gradient_less_table_pl_kernel(tc, g, wd_words, wd_scales, tb, wu_words, wu_scales, offs, offs2, out_0, out_1, out_2):
+    nc = tc.nc
+    with ExitStack() as ctx:
+        pool = ctx.enter_context(tc.tile_pool(name="sbuf", bufs=1))
+        psum = ctx.enter_context(tc.psum_pool(name="psum", bufs=1))
+
+        g_list = pool.tile([P, J // 16], U16, name="g_list")
+        tb_list = pool.tile([P, J // 16], U16, name="tb_list")
+
+        wd_raw = pool.tile([P, C], I32, name="wd_raw")
+        wu_raw = pool.tile([P, 2 * C], U8, name="wu_raw")
+        nc.sync.dma_start(out=wd_raw[:], in_=wd_words[0].rearrange("p c r -> p (c r)").bitcast(I32))
+        nc.sync.dma_start(out=wu_raw[:].bitcast(I32), in_=wu_words[0].bitcast(I32))
+
+        wd_sraw = pool.tile([P, C], U8, name="wd_sraw")
+        wu_sraw = pool.tile([P, C], U8, name="wu_sraw")
+        load_scale_rows(nc, nc.scalar, wd_sraw, wd_scales)
+
+        g_rows = g.rearrange("(p t) c -> p t c", t=PACK)
+        g_raw = {}
+        for h in range(2):
+            for c in range(2):
+                g_raw[h, c] = pool.tile([P, 2, HALF_T], F32, name="g_raw%d%d" % (h, c))
+                nc.sync.dma_start(out=g_raw[h, c][:], in_=g_rows[:, 2 * h : 2 * h + 2, c * HALF_T : (c + 1) * HALF_T])
+            if h == 0:
+                nc.sync.dma_start(g_list[:], offs)
+
+        load_scale_rows(nc, nc.sync, wu_sraw, wu_scales)
+
+        tb_rows = tb.rearrange("(p t) c -> p t c", t=PACK)
+        tb_win = []
+        for t in range(PACK):
+            tb_win.append(pool.tile([P, T], F32, name="tb_win%d" % t))
+            nc.sync.dma_start(out=tb_win[t][:], in_=tb_rows[:, t, :])
+            if t == 0:
+                nc.sync.dma_start(tb_list[:], offs2)
+
+        wd_codes = pool.tile([P, C], I32, name="wd_codes", align_bytes=64)
+        wu_codes = pool.tile([P, 2 * C], U8, name="wu_codes", align_bytes=64)
+        wd_plane = pool.tile([P, C], U8, name="wd_plane", align_bytes=64)
+        wu_plane = pool.tile([P, C], U8, name="wu_plane", align_bytes=64)
+        deal(nc, wd_codes[:], wd_raw[:], 1)
+        deal(nc, wu_codes[:], wu_raw[:], 2)
+
+        g_woven = pool.tile([P, J * PACK], BF16, name="g_woven", tag="woven_then_picked", align_bytes=64)
+        g_woven_words = g_woven[:].bitcast(U32).rearrange("p (j h) -> p j h", h=2)
+        for h in range(2):
+            g_win = pool.tile([P, T], U32, name="g_win%d" % h)
+            pairs = g_win[:].bitcast(BF16).rearrange("p (c e) -> p c e", e=2)
+            first = g_raw[h, 0][:].rearrange("p e c -> p c e")
+            second = g_raw[h, 1][:].rearrange("p e c -> p c e")
+            nc.scalar.activation(out=pairs[:, 0:HALF_T, :], in_=first, func=COPY)
+            split = HALF_T if h == 0 else LAST_CAST_VECTOR
+            nc.vector.tensor_copy(out=pairs[:, HALF_T : HALF_T + split, :], in_=second[:, 0:split, :])
+            if split < HALF_T:
+                nc.scalar.activation(out=pairs[:, HALF_T + split : T, :], in_=second[:, split:HALF_T, :], func=COPY)
+            nc.vector.tensor_copy(out=g_woven_words[:, :, h], in_=g_win[:].indirect(g_list[:]))
+            if h == 0:
+                deal(nc, wd_plane[:], wd_sraw[:], 1)
+            else:
+                deal(nc, wu_plane[:], wu_sraw[:], 1)
+
+        g_codes = pool.tile([P, J], U32, name="g_codes", align_bytes=64)
+        g_plane = pool.tile([P, J], U8, name="g_plane", align_bytes=64)
+        nc.vector.quantize_mx(out=g_codes[:].bitcast(E5M2), scales=g_plane[:], in_=g_woven[:])
+
+        neg_dz = pool.tile([P, PACK, J], F32, name="neg_dz")
+        dz_woven = pool.tile([P, J, PACK], BF16, name="dz_woven", align_bytes=64)
+        neg_dz_cols = neg_dz[:].rearrange("p t j -> p j t")
+        for t in range(PACK):
+            dh = psum.tile([P, J], F32, name="dh%d" % t)
+            cols = slice(t * P, (t + 1) * P)
+            nc.tensor.matmul_mx(
+                out=dh[:],
+                lhsT=wd_codes[:, cols].bitcast(E4M3),
+                lhsT_scale=wd_plane[:, cols],
+                rhs=g_codes[:].bitcast(E5M2),
+                rhs_scale=g_plane[:],
+                start=True,
+                stop=True,
+            )
+            if t == 0:
+                tb_picked = pool.tile([P, J], F32, name="tb_picked", tag="woven_then_picked", align_bytes=64)
+                nc.vector.tensor_copy(out=tb_picked[:], in_=tb_win[t][:].indirect(tb_list[:]))
+                nc.vector.tensor_tensor(out=neg_dz[:, t, :], in0=tb_picked[:], in1=dh[:], op=SUB)
+            else:
+                dh_sb = pool.tile([P, J], F32, name="dh_sb%d" % t)
+                nc.scalar.copy(out=dh_sb[:], in_=dh[:])
+                nc.vector.tensor_tensor(out=neg_dz[:, t, :], in0=tb_win[t][:].indirect(tb_list[:]), in1=dh_sb[:], op=SUB)
+        nc.scalar.activation(out=dz_woven[:, :, 0:2], in_=neg_dz_cols[:, :, 0:2], func=COPY, scale=-1.0)
+        for a, b in ((0, HALF_J), (HALF_J, PAIR_VECTOR)):
+            nc.vector.tensor_scalar(out=dz_woven[:, a:b, 2:4], in0=neg_dz_cols[:, a:b, 2:4], scalar1=-1.0, scalar2=None, op0=MULT)
+        nc.scalar.activation(out=dz_woven[:, PAIR_VECTOR:J, 2:4], in_=neg_dz_cols[:, PAIR_VECTOR:J, 2:4], func=COPY, scale=-1.0)
+
+        dz_codes = pool.tile([P, J], U32, name="dz_codes", align_bytes=64)
+        dz_plane = pool.tile([P, J], U8, name="dz_plane", align_bytes=64)
+        for c in range(2):
+            js = slice(c * HALF_J, (c + 1) * HALF_J)
+            nc.vector.quantize_mx(
+                out=dz_codes[:, js].bitcast(E5M2),
+                scales=dz_plane[:, js],
+                in_=dz_woven[:, js, :].rearrange("p j t -> p (j t)"),
+            )
+
+        y = pool.tile([P, PACK, J], F32, name="y")
+        y_cols = y[:].rearrange("p t j -> p j t")
+        y_woven = pool.tile([P, J, PACK], BF16, name="y_woven", align_bytes=64)
+        y_rows = out_0.rearrange("(p t) j -> p t j", t=PACK)
+        for t in range(PACK):
+            acc = psum.tile([P, J], F32, name="acc%d" % t)
+            nc.tensor.matmul_mx(
+                out=acc[:],
+                lhsT=wu_codes[:, 2 * t * P : 2 * (t + 1) * P].bitcast(E2M1),
+                lhsT_scale=wu_plane[:, t * P : (t + 1) * P],
+                rhs=dz_codes[:].bitcast(E5M2),
+                rhs_scale=dz_plane[:],
+                start=True,
+                stop=True,
+            )
+            nc.scalar.copy(out=y[:, t, :], in_=acc[:])
+            nc.sync.dma_start(out=y_rows[:, t, :], in_=y[:, t, :])
+            if t == 1:
+                nc.vector.tensor_copy(out=y_woven[:, :, 0:2], in_=y_cols[:, :, 0:2])
+        for a, b in ((0, HALF_J), (HALF_J, PAIR_VECTOR)):
+            nc.vector.tensor_copy(out=y_woven[:, a:b, 2:4], in_=y_cols[:, a:b, 2:4])
+        nc.scalar.copy(out=y_woven[:, PAIR_VECTOR:J, 2:4], in_=y_cols[:, PAIR_VECTOR:J, 2:4])
+
+        y_codes = pool.tile([P, J], U32, name="y_codes", align_bytes=64)
+        y_plane = pool.tile([P, J], U8, name="y_plane", align_bytes=64)
+        word_rows = out_1[0].rearrange("p c r -> p (c r)").bitcast(I32)
+        for c in range(2):
+            js = slice(c * HALF_J, (c + 1) * HALF_J)
+            nc.vector.quantize_mx(
+                out=y_codes[:, js].bitcast(E4M3),
+                scales=y_plane[:, js],
+                in_=y_woven[:, js, :].rearrange("p j t -> p (j t)"),
+            )
+            nc.sync.dma_start(out=word_rows[:, js], in_=y_codes[:, js].bitcast(I32))
+        for q in range(4):
+            queue = nc.scalar if q % 2 == 0 else nc.sync
+            queue.dma_start(out=out_2[0, 4 * q : 4 * q + 4, :].bitcast(I32), in_=y_plane[32 * q : 32 * q + 4, :].bitcast(I32))

@@ -23,15 +23,17 @@ C = 512
 HALF_T = T // 2
 HALF_J = J // 2
 LAST_CAST_VECTOR = 352
-PAIR_VECTOR = 352
+PAIR_VECTOR = 384
+DZ_FIRST = 320
+DZ_VECTOR = 448
 
 FLOPS = 2 * 2 * 512 * 512 * 512
 
 
-def load_scale_rows(nc, queue, tile, rows):
-    nc.vector.memset(tile[:].bitcast(U32), 0)
+def load_scale_rows(nc, tile, rows):
+    nc.gpsimd.memset(tile[:].bitcast(U32), 0)
     for q in range(4):
-        queue.dma_start(out=tile[32 * q : 32 * q + 4, :].bitcast(I32), in_=rows[0, 4 * q : 4 * q + 4, :].bitcast(I32))
+        nc.sync.dma_start(out=tile[32 * q : 32 * q + 4, :].bitcast(I32), in_=rows[0, 4 * q : 4 * q + 4, :].bitcast(I32))
 
 
 def deal(nc, dealt, raw, b):
@@ -52,12 +54,10 @@ def tile_list_gradient_less_table_pl_kernel(tc, g, wd_words, wd_scales, tb, wu_w
 
         wd_raw = pool.tile([P, C], I32, name="wd_raw")
         wu_raw = pool.tile([P, 2 * C], U8, name="wu_raw")
-        nc.sync.dma_start(out=wd_raw[:], in_=wd_words[0].rearrange("p c r -> p (c r)").bitcast(I32))
-        nc.sync.dma_start(out=wu_raw[:].bitcast(I32), in_=wu_words[0].bitcast(I32))
 
         wd_sraw = pool.tile([P, C], U8, name="wd_sraw")
         wu_sraw = pool.tile([P, C], U8, name="wu_sraw")
-        load_scale_rows(nc, nc.scalar, wd_sraw, wd_scales)
+        load_scale_rows(nc, wd_sraw, wd_scales)
 
         g_rows = g.rearrange("(p t) c -> p t c", t=PACK)
         g_raw = {}
@@ -65,25 +65,24 @@ def tile_list_gradient_less_table_pl_kernel(tc, g, wd_words, wd_scales, tb, wu_w
             for c in range(2):
                 g_raw[h, c] = pool.tile([P, 2, HALF_T], F32, name="g_raw%d%d" % (h, c))
                 nc.sync.dma_start(out=g_raw[h, c][:], in_=g_rows[:, 2 * h : 2 * h + 2, c * HALF_T : (c + 1) * HALF_T])
-            if h == 0:
-                nc.sync.dma_start(g_list[:], offs)
-
-        load_scale_rows(nc, nc.sync, wu_sraw, wu_scales)
+                if h == 0 and c == 0:
+                    nc.sync.dma_start(g_list[:], offs)
+        nc.sync.dma_start(out=wd_raw[:], in_=wd_words[0].rearrange("p c r -> p (c r)").bitcast(I32))
 
         tb_rows = tb.rearrange("(p t) c -> p t c", t=PACK)
         tb_win = []
         for t in range(PACK):
-            tb_win.append(pool.tile([P, T], F32, name="tb_win%d" % t))
+            tb_win.append(pool.tile([P, T], F32, name="tb_win%d" % t, tag="tb_win%d" % t, align_bytes=64))
             nc.sync.dma_start(out=tb_win[t][:], in_=tb_rows[:, t, :])
             if t == 0:
                 nc.sync.dma_start(tb_list[:], offs2)
+            if t == 1:
+                nc.sync.dma_start(out=wu_raw[:].bitcast(I32), in_=wu_words[0].bitcast(I32))
+
+        load_scale_rows(nc, wu_sraw, wu_scales)
 
         wd_codes = pool.tile([P, C], I32, name="wd_codes", align_bytes=64)
-        wu_codes = pool.tile([P, 2 * C], U8, name="wu_codes", align_bytes=64)
         wd_plane = pool.tile([P, C], U8, name="wd_plane", align_bytes=64)
-        wu_plane = pool.tile([P, C], U8, name="wu_plane", align_bytes=64)
-        deal(nc, wd_codes[:], wd_raw[:], 1)
-        deal(nc, wu_codes[:], wu_raw[:], 2)
 
         g_woven = pool.tile([P, J * PACK], BF16, name="g_woven", tag="woven_then_picked", align_bytes=64)
         g_woven_words = g_woven[:].bitcast(U32).rearrange("p (j h) -> p j h", h=2)
@@ -101,14 +100,15 @@ def tile_list_gradient_less_table_pl_kernel(tc, g, wd_words, wd_scales, tb, wu_w
             if h == 0:
                 deal(nc, wd_plane[:], wd_sraw[:], 1)
             else:
-                deal(nc, wu_plane[:], wu_sraw[:], 1)
+                deal(nc, wd_codes[:], wd_raw[:], 1)
 
         g_codes = pool.tile([P, J], U32, name="g_codes", align_bytes=64)
         g_plane = pool.tile([P, J], U8, name="g_plane", align_bytes=64)
         nc.vector.quantize_mx(out=g_codes[:].bitcast(E5M2), scales=g_plane[:], in_=g_woven[:])
 
         neg_dz = pool.tile([P, PACK, J], F32, name="neg_dz")
-        dz_woven = pool.tile([P, J, PACK], BF16, name="dz_woven", align_bytes=64)
+        dz_woven = pool.tile([P, J, PACK], BF16, name="dz_woven", tag="dz_woven", align_bytes=64)
+        dh_sb = {}
         neg_dz_cols = neg_dz[:].rearrange("p t j -> p j t")
         for t in range(PACK):
             dh = psum.tile([P, J], F32, name="dh%d" % t)
@@ -125,15 +125,27 @@ def tile_list_gradient_less_table_pl_kernel(tc, g, wd_words, wd_scales, tb, wu_w
             if t == 0:
                 tb_picked = pool.tile([P, J], F32, name="tb_picked", tag="woven_then_picked", align_bytes=64)
                 nc.vector.tensor_copy(out=tb_picked[:], in_=tb_win[t][:].indirect(tb_list[:]))
+                wu_codes = pool.tile([P, 2 * C], U8, name="wu_codes", tag="tb_win0", align_bytes=64)
+                deal(nc, wu_codes[:].bitcast(U16), wu_raw[:].bitcast(U16), 1)
                 nc.vector.tensor_tensor(out=neg_dz[:, t, :], in0=tb_picked[:], in1=dh[:], op=SUB)
             else:
-                dh_sb = pool.tile([P, J], F32, name="dh_sb%d" % t)
-                nc.scalar.copy(out=dh_sb[:], in_=dh[:])
-                nc.vector.tensor_tensor(out=neg_dz[:, t, :], in0=tb_win[t][:].indirect(tb_list[:]), in1=dh_sb[:], op=SUB)
+                dh_sb[t] = pool.tile([P, J], F32, name="dh_sb%d" % t)
+                nc.scalar.copy(out=dh_sb[t][:], in_=dh[:])
+
+        def picked_less_dh(t, a, b):
+            nc.vector.tensor_tensor(out=neg_dz[:, t, a:b], in0=tb_win[t][:].indirect(tb_list[:, a // 16 : b // 16]), in1=dh_sb[t][:, a:b], op=SUB)
+
+        picked_less_dh(1, 0, J)
         nc.scalar.activation(out=dz_woven[:, :, 0:2], in_=neg_dz_cols[:, :, 0:2], func=COPY, scale=-1.0)
-        for a, b in ((0, HALF_J), (HALF_J, PAIR_VECTOR)):
-            nc.vector.tensor_scalar(out=dz_woven[:, a:b, 2:4], in0=neg_dz_cols[:, a:b, 2:4], scalar1=-1.0, scalar2=None, op0=MULT)
-        nc.scalar.activation(out=dz_woven[:, PAIR_VECTOR:J, 2:4], in_=neg_dz_cols[:, PAIR_VECTOR:J, 2:4], func=COPY, scale=-1.0)
+        for a, b in ((0, DZ_FIRST), (DZ_FIRST, J)):
+            picked_less_dh(2, a, b)
+            picked_less_dh(3, a, b)
+        nc.scalar.activation(out=dz_woven[:, 0:DZ_FIRST, 2:4], in_=neg_dz_cols[:, 0:DZ_FIRST, 2:4], func=COPY, scale=-1.0)
+        nc.vector.tensor_scalar(out=dz_woven[:, DZ_FIRST:DZ_VECTOR, 2:4], in0=neg_dz_cols[:, DZ_FIRST:DZ_VECTOR, 2:4], scalar1=-1.0, scalar2=None, op0=MULT)
+        nc.scalar.activation(out=dz_woven[:, DZ_VECTOR:J, 2:4], in_=neg_dz_cols[:, DZ_VECTOR:J, 2:4], func=COPY, scale=-1.0)
+
+        wu_plane_first = pool.tile([P, P], U8, name="wu_plane_first", tag="tb_win1", align_bytes=64)
+        nc.vector.tensor_copy(out=wu_plane_first[:], in_=wu_sraw[:].rearrange("p (m t) -> p t m", t=PACK)[:, 0, :])
 
         dz_codes = pool.tile([P, J], U32, name="dz_codes", align_bytes=64)
         dz_plane = pool.tile([P, J], U8, name="dz_plane", align_bytes=64)
@@ -145,6 +157,12 @@ def tile_list_gradient_less_table_pl_kernel(tc, g, wd_words, wd_scales, tb, wu_w
                 in_=dz_woven[:, js, :].rearrange("p j t -> p (j t)"),
             )
 
+        wu_plane_rest = pool.tile([P, PACK - 1, P], U8, name="wu_plane_rest", tag="dz_woven", align_bytes=64)
+        nc.vector.tensor_copy(
+            out=wu_plane_rest[:].rearrange("p t m -> p m t"),
+            in_=wu_sraw[:].rearrange("p (m t) -> p m t", t=PACK)[:, :, 1:PACK],
+        )
+
         y = pool.tile([P, PACK, J], F32, name="y")
         y_cols = y[:].rearrange("p t j -> p j t")
         y_woven = pool.tile([P, J, PACK], BF16, name="y_woven", align_bytes=64)
@@ -154,17 +172,18 @@ def tile_list_gradient_less_table_pl_kernel(tc, g, wd_words, wd_scales, tb, wu_w
             nc.tensor.matmul_mx(
                 out=acc[:],
                 lhsT=wu_codes[:, 2 * t * P : 2 * (t + 1) * P].bitcast(E2M1),
-                lhsT_scale=wu_plane[:, t * P : (t + 1) * P],
+                lhsT_scale=wu_plane_first[:] if t == 0 else wu_plane_rest[:, t - 1, :],
                 rhs=dz_codes[:].bitcast(E5M2),
                 rhs_scale=dz_plane[:],
                 start=True,
                 stop=True,
             )
-            nc.scalar.copy(out=y[:, t, :], in_=acc[:])
+            for a, b in ((0, J),) if t < PACK - 1 else ((0, P), (P, HALF_J), (HALF_J, J)):
+                nc.scalar.copy(out=y[:, t, a:b], in_=acc[:, a:b])
             nc.sync.dma_start(out=y_rows[:, t, :], in_=y[:, t, :])
             if t == 1:
                 nc.vector.tensor_copy(out=y_woven[:, :, 0:2], in_=y_cols[:, :, 0:2])
-        for a, b in ((0, HALF_J), (HALF_J, PAIR_VECTOR)):
+        for a, b in ((0, P), (P, HALF_J), (HALF_J, PAIR_VECTOR)):
             nc.vector.tensor_copy(out=y_woven[:, a:b, 2:4], in_=y_cols[:, a:b, 2:4])
         nc.scalar.copy(out=y_woven[:, PAIR_VECTOR:J, 2:4], in_=y_cols[:, PAIR_VECTOR:J, 2:4])
 

@@ -23,9 +23,9 @@ C = 512
 HALF_T = T // 2
 HALF_J = J // 2
 LAST_CAST_VECTOR = 352
-PAIR_VECTOR = 384
-DZ_FIRST = 320
-DZ_VECTOR = 448
+DZ_FIRST = 256
+DZ_VECTOR = 416
+Y_VECTOR = 352
 
 FLOPS = 2 * 2 * 512 * 512 * 512
 
@@ -40,6 +40,13 @@ def deal(nc, dealt, raw, b):
     nc.vector.tensor_copy(
         out=dealt.rearrange("p (t m b) -> p m t b", t=PACK, b=b),
         in_=raw.rearrange("p (m t b) -> p m t b", t=PACK, b=b),
+    )
+
+
+def weave_views(woven, planes, a, b):
+    return (
+        woven[:, a:b, :].rearrange("p (c i) t -> p c t i", i=4),
+        planes[:, :, a:b].rearrange("p t (c i) -> p c t i", i=4),
     )
 
 
@@ -109,7 +116,6 @@ def tile_list_gradient_less_table_pl_kernel(tc, g, wd_words, wd_scales, tb, wu_w
         neg_dz = pool.tile([P, PACK, J], F32, name="neg_dz")
         dz_woven = pool.tile([P, J, PACK], BF16, name="dz_woven", tag="dz_woven", align_bytes=64)
         dh_sb = {}
-        neg_dz_cols = neg_dz[:].rearrange("p t j -> p j t")
         for t in range(PACK):
             dh = psum.tile([P, J], F32, name="dh%d" % t)
             cols = slice(t * P, (t + 1) * P)
@@ -136,13 +142,14 @@ def tile_list_gradient_less_table_pl_kernel(tc, g, wd_words, wd_scales, tb, wu_w
             nc.vector.tensor_tensor(out=neg_dz[:, t, a:b], in0=tb_win[t][:].indirect(tb_list[:, a // 16 : b // 16]), in1=dh_sb[t][:, a:b], op=SUB)
 
         picked_less_dh(1, 0, J)
-        nc.scalar.activation(out=dz_woven[:, :, 0:2], in_=neg_dz_cols[:, :, 0:2], func=COPY, scale=-1.0)
         for a, b in ((0, DZ_FIRST), (DZ_FIRST, J)):
             picked_less_dh(2, a, b)
             picked_less_dh(3, a, b)
-        nc.scalar.activation(out=dz_woven[:, 0:DZ_FIRST, 2:4], in_=neg_dz_cols[:, 0:DZ_FIRST, 2:4], func=COPY, scale=-1.0)
-        nc.vector.tensor_scalar(out=dz_woven[:, DZ_FIRST:DZ_VECTOR, 2:4], in0=neg_dz_cols[:, DZ_FIRST:DZ_VECTOR, 2:4], scalar1=-1.0, scalar2=None, op0=MULT)
-        nc.scalar.activation(out=dz_woven[:, DZ_VECTOR:J, 2:4], in_=neg_dz_cols[:, DZ_VECTOR:J, 2:4], func=COPY, scale=-1.0)
+        for a, b in ((0, DZ_FIRST), (DZ_VECTOR, J)):
+            dst, src = weave_views(dz_woven, neg_dz, a, b)
+            nc.scalar.activation(out=dst, in_=src, func=COPY, scale=-1.0)
+        dst, src = weave_views(dz_woven, neg_dz, DZ_FIRST, DZ_VECTOR)
+        nc.vector.tensor_scalar(out=dst, in0=src, scalar1=-1.0, scalar2=None, op0=MULT)
 
         wu_plane_first = pool.tile([P, P], U8, name="wu_plane_first", tag="tb_win1", align_bytes=64)
         nc.vector.tensor_copy(out=wu_plane_first[:], in_=wu_sraw[:].rearrange("p (m t) -> p t m", t=PACK)[:, 0, :])
@@ -164,7 +171,6 @@ def tile_list_gradient_less_table_pl_kernel(tc, g, wd_words, wd_scales, tb, wu_w
         )
 
         y = pool.tile([P, PACK, J], F32, name="y")
-        y_cols = y[:].rearrange("p t j -> p j t")
         y_woven = pool.tile([P, J, PACK], BF16, name="y_woven", align_bytes=64)
         y_rows = out_0.rearrange("(p t) j -> p t j", t=PACK)
         for t in range(PACK):
@@ -178,14 +184,15 @@ def tile_list_gradient_less_table_pl_kernel(tc, g, wd_words, wd_scales, tb, wu_w
                 start=True,
                 stop=True,
             )
-            for a, b in ((0, J),) if t < PACK - 1 else ((0, P), (P, HALF_J), (HALF_J, J)):
-                nc.scalar.copy(out=y[:, t, a:b], in_=acc[:, a:b])
+            leave = nc.vector.tensor_copy if t % 2 == 0 else nc.scalar.copy
+            for a, b in ((0, J),) if t < PACK - 1 else ((0, HALF_J), (HALF_J, J)):
+                leave(out=y[:, t, a:b], in_=acc[:, a:b])
             nc.sync.dma_start(out=y_rows[:, t, :], in_=y[:, t, :])
-            if t == 1:
-                nc.vector.tensor_copy(out=y_woven[:, :, 0:2], in_=y_cols[:, :, 0:2])
-        for a, b in ((0, P), (P, HALF_J), (HALF_J, PAIR_VECTOR)):
-            nc.vector.tensor_copy(out=y_woven[:, a:b, 2:4], in_=y_cols[:, a:b, 2:4])
-        nc.scalar.copy(out=y_woven[:, PAIR_VECTOR:J, 2:4], in_=y_cols[:, PAIR_VECTOR:J, 2:4])
+        for a, b in ((0, HALF_J), (HALF_J, Y_VECTOR)):
+            dst, src = weave_views(y_woven, y, a, b)
+            nc.vector.tensor_copy(out=dst, in_=src)
+        dst, src = weave_views(y_woven, y, Y_VECTOR, J)
+        nc.scalar.copy(out=dst, in_=src)
 
         y_codes = pool.tile([P, J], U32, name="y_codes", align_bytes=64)
         y_plane = pool.tile([P, J], U8, name="y_plane", align_bytes=64)

@@ -25,7 +25,7 @@ HALF_J = J // 2
 LAST_CAST_VECTOR = 352
 DZ_FIRST = 256
 DZ_VECTOR = 416
-Y_VECTOR = 352
+Y_VECTOR = 384
 
 FLOPS = 2 * 2 * 512 * 512 * 512
 
@@ -79,11 +79,10 @@ def tile_list_gradient_less_table_pl_kernel(tc, g, wd_words, wd_scales, tb, wu_w
         tb_rows = tb.rearrange("(p t) c -> p t c", t=PACK)
         tb_win = []
         for t in range(PACK):
-            tb_win.append(pool.tile([P, T], F32, name="tb_win%d" % t, tag="tb_win%d" % t, align_bytes=64))
+            tb_win.append(pool.tile([P, T], F32, name="tb_win%d" % t))
             nc.sync.dma_start(out=tb_win[t][:], in_=tb_rows[:, t, :])
             if t == 0:
                 nc.sync.dma_start(tb_list[:], offs2)
-            if t == 1:
                 nc.sync.dma_start(out=wu_raw[:].bitcast(I32), in_=wu_words[0].bitcast(I32))
 
         load_scale_rows(nc, wu_sraw, wu_scales)
@@ -91,7 +90,7 @@ def tile_list_gradient_less_table_pl_kernel(tc, g, wd_words, wd_scales, tb, wu_w
         wd_codes = pool.tile([P, C], I32, name="wd_codes", align_bytes=64)
         wd_plane = pool.tile([P, C], U8, name="wd_plane", align_bytes=64)
 
-        g_woven = pool.tile([P, J * PACK], BF16, name="g_woven", tag="woven_then_picked", align_bytes=64)
+        g_woven = pool.tile([P, J * PACK], BF16, name="g_woven", align_bytes=64)
         g_woven_words = g_woven[:].bitcast(U32).rearrange("p (j h) -> p j h", h=2)
         for h in range(2):
             g_win = pool.tile([P, T], U32, name="g_win%d" % h)
@@ -99,10 +98,9 @@ def tile_list_gradient_less_table_pl_kernel(tc, g, wd_words, wd_scales, tb, wu_w
             first = g_raw[h, 0][:].rearrange("p e c -> p c e")
             second = g_raw[h, 1][:].rearrange("p e c -> p c e")
             nc.scalar.activation(out=pairs[:, 0:HALF_T, :], in_=first, func=COPY)
-            split = HALF_T if h == 0 else LAST_CAST_VECTOR
+            split = LAST_CAST_VECTOR
             nc.vector.tensor_copy(out=pairs[:, HALF_T : HALF_T + split, :], in_=second[:, 0:split, :])
-            if split < HALF_T:
-                nc.scalar.activation(out=pairs[:, HALF_T + split : T, :], in_=second[:, split:HALF_T, :], func=COPY)
+            nc.scalar.activation(out=pairs[:, HALF_T + split : T, :], in_=second[:, split:HALF_T, :], func=COPY)
             nc.vector.tensor_copy(out=g_woven_words[:, :, h], in_=g_win[:].indirect(g_list[:]))
             if h == 0:
                 deal(nc, wd_plane[:], wd_sraw[:], 1)
@@ -117,7 +115,7 @@ def tile_list_gradient_less_table_pl_kernel(tc, g, wd_words, wd_scales, tb, wu_w
         dz_woven = pool.tile([P, J, PACK], BF16, name="dz_woven", tag="dz_woven", align_bytes=64)
         dh_sb = {}
         for t in range(PACK):
-            dh = psum.tile([P, J], F32, name="dh%d" % t)
+            dh = psum.tile([P, J], F32, name="dh%d" % t, tag="dh%d" % t)
             cols = slice(t * P, (t + 1) * P)
             nc.tensor.matmul_mx(
                 out=dh[:],
@@ -129,29 +127,44 @@ def tile_list_gradient_less_table_pl_kernel(tc, g, wd_words, wd_scales, tb, wu_w
                 stop=True,
             )
             if t == 0:
-                tb_picked = pool.tile([P, J], F32, name="tb_picked", tag="woven_then_picked", align_bytes=64)
+                tb_picked = pool.tile([P, J], F32, name="tb_picked")
                 nc.vector.tensor_copy(out=tb_picked[:], in_=tb_win[t][:].indirect(tb_list[:]))
-                wu_codes = pool.tile([P, 2 * C], U8, name="wu_codes", tag="tb_win0", align_bytes=64)
+                wu_codes = pool.tile([P, 2 * C], U8, name="wu_codes", align_bytes=64)
                 deal(nc, wu_codes[:].bitcast(U16), wu_raw[:].bitcast(U16), 1)
                 nc.vector.tensor_tensor(out=neg_dz[:, t, :], in0=tb_picked[:], in1=dh[:], op=SUB)
-            else:
+            elif t < PACK - 1:
                 dh_sb[t] = pool.tile([P, J], F32, name="dh_sb%d" % t)
                 nc.scalar.copy(out=dh_sb[t][:], in_=dh[:])
+            else:
+                last_dh = dh
 
-        def picked_less_dh(t, a, b):
-            nc.vector.tensor_tensor(out=neg_dz[:, t, a:b], in0=tb_win[t][:].indirect(tb_list[:, a // 16 : b // 16]), in1=dh_sb[t][:, a:b], op=SUB)
+        def picked_less_dh(t, a, b, dh_cols):
+            nc.vector.tensor_tensor(out=neg_dz[:, t, a:b], in0=tb_win[t][:].indirect(tb_list[:, a // 16 : b // 16]), in1=dh_cols, op=SUB)
 
-        picked_less_dh(1, 0, J)
+        picked_less_dh(1, 0, J, dh_sb[1][:])
         for a, b in ((0, DZ_FIRST), (DZ_FIRST, J)):
-            picked_less_dh(2, a, b)
-            picked_less_dh(3, a, b)
+            last_dh_half = pool.tile([P, b - a], F32, name="last_dh_half")
+            nc.scalar.copy(out=last_dh_half[:], in_=last_dh[:, a:b])
+            picked_less_dh(2, a, b, dh_sb[2][:, a:b])
+            picked_less_dh(3, a, b, last_dh_half[:])
+        warm = psum.tile([P, J], F32, name="warm", tag="dh3")
+        for r in range(2):
+            nc.tensor.matmul_mx(
+                out=warm[:],
+                lhsT=wd_codes[:, 0:P].bitcast(E4M3),
+                lhsT_scale=wd_plane[:, 0:P],
+                rhs=g_codes[:].bitcast(E5M2),
+                rhs_scale=g_plane[:],
+                start=True,
+                stop=True,
+            )
         for a, b in ((0, DZ_FIRST), (DZ_VECTOR, J)):
             dst, src = weave_views(dz_woven, neg_dz, a, b)
             nc.scalar.activation(out=dst, in_=src, func=COPY, scale=-1.0)
         dst, src = weave_views(dz_woven, neg_dz, DZ_FIRST, DZ_VECTOR)
         nc.vector.tensor_scalar(out=dst, in0=src, scalar1=-1.0, scalar2=None, op0=MULT)
 
-        wu_plane_first = pool.tile([P, P], U8, name="wu_plane_first", tag="tb_win1", align_bytes=64)
+        wu_plane_first = pool.tile([P, P], U8, name="wu_plane_first", align_bytes=64)
         nc.vector.tensor_copy(out=wu_plane_first[:], in_=wu_sraw[:].rearrange("p (m t) -> p t m", t=PACK)[:, 0, :])
 
         dz_codes = pool.tile([P, J], U32, name="dz_codes", align_bytes=64)
@@ -185,10 +198,10 @@ def tile_list_gradient_less_table_pl_kernel(tc, g, wd_words, wd_scales, tb, wu_w
                 stop=True,
             )
             leave = nc.vector.tensor_copy if t % 2 == 0 else nc.scalar.copy
-            for a, b in ((0, J),) if t < PACK - 1 else ((0, HALF_J), (HALF_J, J)):
+            for a, b in ((0, J),) if t < PACK - 1 else ((0, P), (P, HALF_J), (HALF_J, J)):
                 leave(out=y[:, t, a:b], in_=acc[:, a:b])
             nc.sync.dma_start(out=y_rows[:, t, :], in_=y[:, t, :])
-        for a, b in ((0, HALF_J), (HALF_J, Y_VECTOR)):
+        for a, b in ((0, P), (P, HALF_J), (HALF_J, Y_VECTOR)):
             dst, src = weave_views(y_woven, y, a, b)
             nc.vector.tensor_copy(out=dst, in_=src)
         dst, src = weave_views(y_woven, y, Y_VECTOR, J)

@@ -147,17 +147,6 @@ def tile_list_gradient_less_table_pl_kernel(tc, g, wd_words, wd_scales, tb, wu_w
             nc.scalar.copy(out=last_dh_half[:], in_=last_dh[:, a:b])
             picked_less_dh(2, a, b, dh_sb[2][:, a:b])
             picked_less_dh(3, a, b, last_dh_half[:])
-        warm = psum.tile([P, J], F32, name="warm", tag="dh3")
-        for r in range(2):
-            nc.tensor.matmul_mx(
-                out=warm[:],
-                lhsT=wd_codes[:, 0:P].bitcast(E4M3),
-                lhsT_scale=wd_plane[:, 0:P],
-                rhs=g_codes[:].bitcast(E5M2),
-                rhs_scale=g_plane[:],
-                start=True,
-                stop=True,
-            )
         for a, b in ((0, DZ_FIRST), (DZ_VECTOR, J)):
             dst, src = weave_views(dz_woven, neg_dz, a, b)
             nc.scalar.activation(out=dst, in_=src, func=COPY, scale=-1.0)

from contextlib import ExitStack

import concourse.mybir as mybir

F32 = mybir.dt.float32
BF16 = mybir.dt.bfloat16
I32 = mybir.dt.int32
U32 = mybir.dt.uint32
U16 = mybir.dt.uint16
U8 = mybir.dt.uint8
E4M3 = mybir.dt.float8_e4m3fn_x4
E5M2 = mybir.dt.float8_e5m2_x4
E2M1 = mybir.dt.float4_e2m1fn_x4
COPY = mybir.ActivationFunctionType.Copy
MULT = mybir.AluOpType.mult
SUB = mybir.AluOpType.subtract

P = 128
PACK = 4
T = 1024
J = 512
C = 512
HALF_T = T // 2
HALF_J = J // 2
LAST_CAST_VECTOR = 352
DZ_FIRST = 256
DZ_VECTOR = 416
Y_VECTOR = 384

FLOPS = 2 * 2 * 512 * 512 * 512


def load_scale_rows(nc, tile, rows):
    nc.gpsimd.memset(tile[:].bitcast(U32), 0)
    for q in range(4):
        nc.sync.dma_start(out=tile[32 * q : 32 * q + 4, :].bitcast(I32), in_=rows[0, 4 * q : 4 * q + 4, :].bitcast(I32))


def deal(nc, dealt, raw, b):
    nc.vector.tensor_copy(
        out=dealt.rearrange("p (t m b) -> p m t b", t=PACK, b=b),
        in_=raw.rearrange("p (m t b) -> p m t b", t=PACK, b=b),
    )


def weave_views(woven, planes, a, b):
    return (
        woven[:, a:b, :].rearrange("p (c i) t -> p c t i", i=4),
        planes[:, :, a:b].rearrange("p t (c i) -> p c t i", i=4),
    )


def tile_list_gradient_less_table_pl_kernel(tc, g, wd_words, wd_scales, tb, wu_words, wu_scales, offs, offs2, out_0, out_1, out_2):
    nc = tc.nc
    with ExitStack() as ctx:
        pool = ctx.enter_context(tc.tile_pool(name="sbuf", bufs=1))
        psum = ctx.enter_context(tc.psum_pool(name="psum", bufs=1))

        g_list = pool.tile([P, J // 16], U16, name="g_list")
        tb_list = pool.tile([P, J // 16], U16, name="tb_list")

        wd_raw = pool.tile([P, C], I32, name="wd_raw")
        wu_raw = pool.tile([P, 2 * C], U8, name="wu_raw")

        wd_sraw = pool.tile([P, C], U8, name="wd_sraw")
        wu_sraw = pool.tile([P, C], U8, name="wu_sraw")
        load_scale_rows(nc, wd_sraw, wd_scales)

        g_rows = g.rearrange("(p t) c -> p t c", t=PACK)
        g_raw = {}
        for h in range(2):
            for c in range(2):
                g_raw[h, c] = pool.tile([P, 2, HALF_T], F32, name="g_raw%d%d" % (h, c))
                nc.sync.dma_start(out=g_raw[h, c][:], in_=g_rows[:, 2 * h : 2 * h + 2, c * HALF_T : (c + 1) * HALF_T])
                if h == 0 and c == 0:
                    nc.sync.dma_start(g_list[:], offs)
        nc.sync.dma_start(out=wd_raw[:], in_=wd_words[0].rearrange("p c r -> p (c r)").bitcast(I32))

        tb_rows = tb.rearrange("(p t) c -> p t c", t=PACK)
        tb_win = []
        for t in range(PACK):
            tb_win.append(pool.tile([P, T], F32, name="tb_win%d" % t))
            nc.sync.dma_start(out=tb_win[t][:], in_=tb_rows[:, t, :])
            if t == 0:
                nc.sync.dma_start(tb_list[:], offs2)
                nc.sync.dma_start(out=wu_raw[:].bitcast(I32), in_=wu_words[0].bitcast(I32))

        load_scale_rows(nc, wu_sraw, wu_scales)

        wd_codes = pool.tile([P, C], I32, name="wd_codes", align_bytes=64)
        wd_plane = pool.tile([P, C], U8, name="wd_plane", align_bytes=64)

        g_woven = pool.tile([P, J * PACK], BF16, name="g_woven", align_bytes=64)
        g_woven_words = g_woven[:].bitcast(U32).rearrange("p (j h) -> p j h", h=2)
        for h in range(2):
            g_win = pool.tile([P, T], U32, name="g_win%d" % h)
            pairs = g_win[:].bitcast(BF16).rearrange("p (c e) -> p c e", e=2)
            first = g_raw[h, 0][:].rearrange("p e c -> p c e")
            second = g_raw[h, 1][:].rearrange("p e c -> p c e")
            nc.scalar.activation(out=pairs[:, 0:HALF_T, :], in_=first, func=COPY)
            split = LAST_CAST_VECTOR
            nc.vector.tensor_copy(out=pairs[:, HALF_T : HALF_T + split, :], in_=second[:, 0:split, :])
            nc.scalar.activation(out=pairs[:, HALF_T + split : T, :], in_=second[:, split:HALF_T, :], func=COPY)
            nc.vector.tensor_copy(out=g_woven_words[:, :, h], in_=g_win[:].indirect(g_list[:]))
            if h == 0:
                deal(nc, wd_plane[:], wd_sraw[:], 1)
            else:
                deal(nc, wd_codes[:], wd_raw[:], 1)

        g_codes = pool.tile([P, J], U32, name="g_codes", align_bytes=64)
        g_plane = pool.tile([P, J], U8, name="g_plane", align_bytes=64)
        nc.vector.quantize_mx(out=g_codes[:].bitcast(E5M2), scales=g_plane[:], in_=g_woven[:])

        neg_dz = pool.tile([P, PACK, J], F32, name="neg_dz")
        dz_woven = pool.tile([P, J, PACK], BF16, name="dz_woven", tag="dz_woven", align_bytes=64)
        dh_sb = {}
        for t in range(PACK):
            dh = psum.tile([P, J], F32, name="dh%d" % t, tag="dh%d" % t)
            cols = slice(t * P, (t + 1) * P)
            nc.tensor.matmul_mx(
                out=dh[:],
                lhsT=wd_codes[:, cols].bitcast(E4M3),
                lhsT_scale=wd_plane[:, cols],
                rhs=g_codes[:].bitcast(E5M2),
                rhs_scale=g_plane[:],
                start=True,
                stop=True,
            )
            if t == 0:
                tb_picked = pool.tile([P, J], F32, name="tb_picked")
                nc.vector.tensor_copy(out=tb_picked[:], in_=tb_win[t][:].indirect(tb_list[:]))
                wu_codes = pool.tile([P, 2 * C], U8, name="wu_codes", align_bytes=64)
                deal(nc, wu_codes[:].bitcast(U16), wu_raw[:].bitcast(U16), 1)
                nc.vector.tensor_tensor(out=neg_dz[:, t, :], in0=tb_picked[:], in1=dh[:], op=SUB)
            elif t < PACK - 1:
                dh_sb[t] = pool.tile([P, J], F32, name="dh_sb%d" % t)
                nc.scalar.copy(out=dh_sb[t][:], in_=dh[:])
            else:
                last_dh = dh

        def picked_less_dh(t, a, b, dh_cols):
            nc.vector.tensor_tensor(out=neg_dz[:, t, a:b], in0=tb_win[t][:].indirect(tb_list[:, a // 16 : b // 16]), in1=dh_cols, op=SUB)

        picked_less_dh(1, 0, J, dh_sb[1][:])
        for a, b in ((0, DZ_FIRST), (DZ_FIRST, J)):
            last_dh_half = pool.tile([P, b - a], F32, name="last_dh_half")
            nc.scalar.copy(out=last_dh_half[:], in_=last_dh[:, a:b])
            picked_less_dh(2, a, b, dh_sb[2][:, a:b])
            picked_less_dh(3, a, b, last_dh_half[:])
        for a, b in ((0, DZ_FIRST), (DZ_VECTOR, J)):
            dst, src = weave_views(dz_woven, neg_dz, a, b)
            nc.scalar.activation(out=dst, in_=src, func=COPY, scale=-1.0)
        dst, src = weave_views(dz_woven, neg_dz, DZ_FIRST, DZ_VECTOR)
        nc.vector.tensor_scalar(out=dst, in0=src, scalar1=-1.0, scalar2=None, op0=MULT)

        wu_plane_first = pool.tile([P, P], U8, name="wu_plane_first", align_bytes=64)
        nc.vector.tensor_copy(out=wu_plane_first[:], in_=wu_sraw[:].rearrange("p (m t) -> p t m", t=PACK)[:, 0, :])

        dz_codes = pool.tile([P, J], U32, name="dz_codes", align_bytes=64)
        dz_plane = pool.tile([P, J], U8, name="dz_plane", align_bytes=64)
        for c in range(2):
            js = slice(c * HALF_J, (c + 1) * HALF_J)
            nc.vector.quantize_mx(
                out=dz_codes[:, js].bitcast(E5M2),
                scales=dz_plane[:, js],
                in_=dz_woven[:, js, :].rearrange("p j t -> p (j t)"),
            )

        wu_plane_rest = pool.tile([P, PACK - 1, P], U8, name="wu_plane_rest", tag="dz_woven", align_bytes=64)
        nc.vector.tensor_copy(
            out=wu_plane_rest[:].rearrange("p t m -> p m t"),
            in_=wu_sraw[:].rearrange("p (m t) -> p m t", t=PACK)[:, :, 1:PACK],
        )

        y = pool.tile([P, PACK, J], F32, name="y")
        y_woven = pool.tile([P, J, PACK], BF16, name="y_woven", align_bytes=64)
        y_rows = out_0.rearrange("(p t) j -> p t j", t=PACK)
        for t in range(PACK):
            acc = psum.tile([P, J], F32, name="acc%d" % t)
            nc.tensor.matmul_mx(
                out=acc[:],
                lhsT=wu_codes[:, 2 * t * P : 2 * (t + 1) * P].bitcast(E2M1),
                lhsT_scale=wu_plane_first[:] if t == 0 else wu_plane_rest[:, t - 1, :],
                rhs=dz_codes[:].bitcast(E5M2),
                rhs_scale=dz_plane[:],
                start=True,
                stop=True,
            )
            leave = nc.vector.tensor_copy if t % 2 == 0 else nc.scalar.copy
            for a, b in ((0, J),) if t < PACK - 1 else ((0, P), (P, HALF_J), (HALF_J, J)):
                leave(out=y[:, t, a:b], in_=acc[:, a:b])
            nc.sync.dma_start(out=y_rows[:, t, :], in_=y[:, t, :])
        for a, b in ((0, P), (P, HALF_J), (HALF_J, Y_VECTOR)):
            dst, src = weave_views(y_woven, y, a, b)
            nc.vector.tensor_copy(out=dst, in_=src)
        dst, src = weave_views(y_woven, y, Y_VECTOR, J)
        nc.scalar.copy(out=dst, in_=src)

        y_codes = pool.tile([P, J], U32, name="y_codes", align_bytes=64)
        y_plane = pool.tile([P, J], U8, name="y_plane", align_bytes=64)
        word_rows = out_1[0].rearrange("p c r -> p (c r)").bitcast(I32)
        for c in range(2):
            js = slice(c * HALF_J, (c + 1) * HALF_J)
            nc.vector.quantize_mx(
                out=y_codes[:, js].bitcast(E4M3),
                scales=y_plane[:, js],
                in_=y_woven[:, js, :].rearrange("p j t -> p (j t)"),
            )
            nc.sync.dma_start(out=word_rows[:, js], in_=y_codes[:, js].bitcast(I32))
        for q in range(4):
            queue = nc.scalar if q % 2 == 0 else nc.sync
            queue.dma_start(out=out_2[0, 4 * q : 4 * q + 4, :].bitcast(I32), in_=y_plane[32 * q : 32 * q + 4, :].bitcast(I32))
